import numpy as np
import ml_dtypes


def mxq(x, axis, fmt="e4m3"):
    dtype, down = {"e4m3": (ml_dtypes.float8_e4m3fn, 7), "e5m2": (ml_dtypes.float8_e5m2, 14)}[fmt]
    v = np.moveaxis(np.asarray(x, np.float32).astype(ml_dtypes.bfloat16).astype(np.float64), axis, -1)
    blocks = v.reshape(v.shape[:-1] + (-1, 32))
    amax = np.abs(blocks).max(-1, keepdims=True)
    byte = np.maximum(np.where(amax > 0, np.frexp(amax)[1] - 1 + 127, 0) - down, 1)
    scale = np.exp2(byte - 127.0)
    codes = (blocks / scale).astype(np.float32).astype(dtype).astype(np.float64)
    return np.moveaxis((codes * scale).reshape(v.shape), -1, axis)


WIDE = False


def mx_kscale(k):
    if not WIDE:
        return np.ones(k)
    levels = np.array([10, -10, 5, -5, 0])
    if k % 512:
        return np.exp2(np.random.permutation(np.resize(levels, k // 32))).repeat(32)
    a = np.empty((k // 512, 16))
    for p in range(k // 512):
        a[p, :8] = np.random.permutation(np.resize(levels, 8))
        for g in range(8):
            far = levels[np.abs(levels - a[p, g]) >= 10]
            a[p, g + 8] = far[np.random.randint(len(far))]
    return np.exp2(a.ravel()).repeat(32)


def f64(x):
    return np.asarray(x).astype(np.float64)


def striped(idx):
    return np.tile(idx.reshape(-1, 16).T, (8, 1)).astype(np.uint16)


def unstriped(offs):
    return offs[:16].T.reshape(-1).astype(np.int64)


def striped8(idx):
    return np.concatenate([x.reshape(-1, 16).T for x in idx]).astype(np.uint16)


def runs(offs, k):
    lists = np.stack([offs[16 * r : 16 * r + 16].T.reshape(-1) for r in range(8)]).astype(np.int64)
    return lists[np.arange(k) % 512 // 64]


def pack_weight(w):
    k, n = w.shape
    w = f64(np.asarray(w, np.float32).astype(ml_dtypes.bfloat16)).reshape(k // 32, 32, n)
    amax = np.abs(w).max(1)
    byte = np.clip(np.where(amax > 0, np.frexp(amax)[1] - 1 + 127 - 7, 1), 1, 254)
    scaled = (w * np.exp2(127.0 - byte)[:, None, :]).reshape(k, n).astype(np.float32)
    words = np.ascontiguousarray(scaled.reshape(k // 512, 128, 4, n).transpose(0, 1, 3, 2)).astype(ml_dtypes.float8_e4m3fn).view(np.uint8)
    return words, np.ascontiguousarray(byte.astype(np.uint8).reshape(k // 512, 16, n))


def unpack_weight(words, scales):
    g, p, n, _ = words.shape
    vals = np.ascontiguousarray(words).view(ml_dtypes.float8_e4m3fn).astype(np.float64) * np.repeat(np.exp2(scales.astype(np.float64) - 127.0), 8, axis=1)[..., None]
    return vals.transpose(0, 1, 3, 2).reshape(g * 512, n)


E2M1 = np.array([0.0, 0.5, 1.0, 1.5, 2.0, 3.0, 4.0, 6.0, -0.0, -0.5, -1.0, -1.5, -2.0, -3.0, -4.0, -6.0])


def pack_fp4(w):
    k, n = w.shape
    w = f64(np.asarray(w, np.float32).astype(ml_dtypes.bfloat16)).reshape(k // 32, 32, n)
    amax = np.abs(w).max(1)
    mant, ex = np.frexp(amax / 6.0)
    byte = np.clip(np.where(amax > 0, np.where(mant > 0.5, ex, ex - 1) + 127, 1), 1, 254)
    scaled = (w * np.exp2(127.0 - byte)[:, None, :]).reshape(k, n).astype(np.float32)
    c = np.ascontiguousarray(scaled.reshape(k // 512, 128, 4, n).transpose(0, 1, 3, 2)).astype(ml_dtypes.float4_e2m1fn).view(np.uint8) & 0xF
    words = (c[..., 0::2] | (c[..., 1::2] << 4)).reshape(k // 512, 128, 2 * n)
    return np.ascontiguousarray(words), np.ascontiguousarray(byte.astype(np.uint8).reshape(k // 512, 16, n))


def unpack_fp4(words, scales):
    g, _, n = scales.shape
    words = np.ascontiguousarray(words).reshape(g, 128, n, 2)
    nib = np.empty((g, 128, n, 4), np.uint8)
    nib[..., 0::2] = words & 0xF
    nib[..., 1::2] = words >> 4
    vals = E2M1[nib] * np.repeat(np.exp2(scales.astype(np.float64) - 127.0), 8, axis=1)[..., None]
    return vals.transpose(0, 1, 3, 2).reshape(g * 512, n)


def planes(y):
    n, m = y.shape
    v = y.astype(np.float32).astype(ml_dtypes.bfloat16).astype(np.float64).reshape(n // 32, 32, m)
    top = np.abs(v).max(1)
    byte = np.clip(np.where(top > 0, np.frexp(top)[1] - 1 + 127 - 7, 1), 1, 254)
    codes = (v * np.exp2(127.0 - byte)[:, None, :]).reshape(n, m).astype(np.float32).astype(ml_dtypes.float8_e4m3fn).view(np.uint8)
    words = codes.reshape(n // 512, 128, 4, m).transpose(0, 1, 3, 2)
    return np.ascontiguousarray(words), np.ascontiguousarray(byte.astype(np.uint8).reshape(n // 512, 16, m))


K, T, S, N, H, W = 512, 2048, 512, 512, 512, 256


def setup_inputs():
    n = np.random.standard_normal
    s = mx_kscale(K)[:, None]
    u = mx_kscale(H)
    packed_xT = pack_weight(n((K, T)) * s)
    packed_w1 = pack_fp4(n((K, H)) / np.sqrt(K) / s)
    packed_w2 = pack_fp4(n((K, H)) / np.sqrt(K) / s)
    packed_w3 = pack_fp4(n((H, N)) / np.sqrt(H) / u[:, None])
    perm = np.stack([np.random.permutation(S) for _ in range(8)])
    return {
        "x_words": packed_xT[0],
        "x_scales": packed_xT[1],
        "w1_words": packed_w1[0],
        "w1_scales": packed_w1[1],
        "w2_words": packed_w2[0],
        "w2_scales": packed_w2[1],
        "gn": (np.random.uniform(0.5, 1.5, (H, 1)) * u[:, None]).astype(np.float32),
        "w3_words": packed_w3[0],
        "w3_scales": packed_w3[1],
        "offs": striped(np.random.permutation(T)[:S]),
        "hz": striped8(np.random.randint(0, T, (8, S))),
        "n1": striped8(np.stack([np.random.permutation(S) for _ in range(8)])),
        "n2": striped8(np.stack([np.random.permutation(S) for _ in range(8)])),
        "n3": striped8(perm[:, :W]),
        "n4": striped8(perm[:, W:]),
    }


def reference(x_words, x_scales, w1_words, w1_scales, w2_words, w2_scales, gn, w3_words, w3_scales, offs, hz, n1, n2, n3, n4):
    xq = unpack_weight(x_words, x_scales)[:, unstriped(offs)]
    y = unpack_fp4(w1_words, w1_scales).T @ xq
    x_hz = unpack_weight(x_words, x_scales)[np.arange(K)[:, None], runs(hz, K)]
    d = unpack_fp4(w2_words, w2_scales).T @ x_hz
    z = f64(gn) * (0.75 * (y * (d[np.arange(H)[:, None], runs(n2, H)]) - ((y[np.arange(H)[:, None], runs(n1, H)]) * d)))
    h = unpack_fp4(w3_words, w3_scales).T @ mxq(z, 0, "e4m3")
    pa = h[np.arange(N)[:, None], runs(n3, N)]
    pb = h[np.arange(N)[:, None], runs(n4, N)]
    rb = pa - pb
    ra = 0.75 * (pa + pb)
    ds = np.zeros((N, S))
    ds[np.arange(N)[:, None], runs(n3, N)] = ra
    out = ds.copy()
    out[np.arange(N)[:, None], runs(n4, N)] = rb
    return (out,) + planes(out)

@@ -1,0 +1,205 @@
+from contextlib import ExitStack
+
+import concourse.mybir as mybir
+
+K, T, S, N, H, W = 512, 2048, 512, 512, 512, 256
+FLOPS = 3 * 2 * 512 * 512 * 512
+
+F32 = mybir.dt.float32
+BF16 = mybir.dt.bfloat16
+I32 = mybir.dt.int32
+U32 = mybir.dt.uint32
+U16 = mybir.dt.uint16
+U8 = mybir.dt.uint8
+FP8X4 = mybir.dt.float8_e4m3fn_x4
+FP4X4 = mybir.dt.float4_e2m1fn_x4
+COPY = mybir.ActivationFunctionType.Copy
+MULT = mybir.AluOpType.mult
+ADD = mybir.AluOpType.add
+SUB = mybir.AluOpType.subtract
+
+P = 128
+PACK = 4
+HALF = S // 2
+
+
+def tile_picked_twhcrossbhaar_none_po_kernel(
+    tc, x_words, x_scales, w1_words, w1_scales, w2_words, w2_scales, gn, w3_words, w3_scales,
+    offs, hz, n1, n2, n3, n4, out_0, out_1, out_2,
+):
+    nc = tc.nc
+    with ExitStack() as ctx:
+        lists = ctx.enter_context(tc.tile_pool(name="lists", bufs=1))
+        sb = ctx.enter_context(tc.tile_pool(name="sb", bufs=1))
+        ps = ctx.enter_context(tc.psum_pool(name="ps", bufs=1))
+
+        def load_list(name, src):
+            tile = lists.tile([P, src.shape[1]], U16, name=name)
+            nc.sync.dma_start(tile[:], src)
+            return tile
+
+        x_scale_rows = sb.tile([P, T], U8, name="x_scale_rows", align_bytes=64)
+        nc.gpsimd.memset(x_scale_rows[:].bitcast(I32), 0)
+        nc.sync.dma_start(x_scale_rows[0:P:8, :].bitcast(I32), x_scales[0].bitcast(I32))
+        hz_t = load_list("hz_t", hz)
+        offs_t = load_list("offs_t", offs)
+        n1_t = load_list("n1_t", n1)
+        n2_t = load_list("n2_t", n2)
+        n3_t = load_list("n3_t", n3)
+        n4_t = load_list("n4_t", n4)
+        x_table = sb.tile([P, T], I32, name="x_table", align_bytes=64)
+        nc.sync.dma_start(x_table[:], x_words[0].rearrange("p n t -> p (n t)").bitcast(I32))
+
+        w_words = (w1_words, w2_words, w3_words)
+        w_raw = [sb.tile([P, 2 * H], U8, name="w_raw%d" % i, align_bytes=64) for i in range(3)]
+        w12_scale_rows = sb.tile([P, 2 * H], U8, name="w12_scale_rows", align_bytes=64)
+        nc.vector.memset(w12_scale_rows[:].bitcast(I32), 0)
+        picked_plane = sb.tile([P, 2 * S], U8, name="picked_plane", align_bytes=64)
+        nc.vector.memset(picked_plane[:].bitcast(I32), 0)
+        w3_scale_rows = sb.tile([P, N], U8, name="w3_scale_rows", align_bytes=64)
+        nc.vector.memset(w3_scale_rows[:].bitcast(I32), 0)
+
+        def load_scale_rows(queue, rows, scales):
+            for q in range(4):
+                queue.dma_start(rows[32 * q : 32 * q + 4, :].bitcast(I32), scales[0, 4 * q : 4 * q + 4, :].bitcast(I32))
+
+        load_scale_rows(nc.sync, w12_scale_rows[:, :H], w1_scales)
+        load_scale_rows(nc.sync, w12_scale_rows[:, H:], w2_scales)
+        gain_in = sb.tile([P, PACK], F32, name="gain_in")
+        for i in range(2):
+            nc.gpsimd.dma_start(w_raw[i][:].bitcast(I32), w_words[i][0].bitcast(I32))
+        nc.gpsimd.dma_start(gain_in[:], gn.rearrange("(p t) o -> p (t o)", t=PACK))
+        nc.gpsimd.dma_start(w_raw[2][:].bitcast(I32), w_words[2][0].bitcast(I32))
+
+        picked_bytes = sb.tile([P, 2 * S], U8, name="picked_bytes", align_bytes=64)
+        nc.vector.tensor_copy(picked_bytes[:, S:], x_scale_rows[:].indirect(hz_t[:]))
+        nc.vector.tensor_copy(picked_bytes[:, :S], x_scale_rows[:].indirect(offs_t[:]))
+        for b in range(4):
+            nc.sync.dma_start(picked_plane[b:P:32, :].bitcast(I32), picked_bytes[8 * b : P : 32, :].bitcast(I32))
+        load_scale_rows(nc.gpsimd, w3_scale_rows[:], w3_scales)
+        gain = sb.tile([P, PACK], F32, name="gain")
+        nc.scalar.activation(gain[:], gain_in[:], COPY, scale=0.75)
+
+        w_codes = [sb.tile([P, 2 * H], U8, name="w_codes%d" % i, align_bytes=64) for i in range(3)]
+
+        def deal_words(i):
+            nc.scalar.copy(
+                w_codes[i][:].bitcast(U16).rearrange("p (t m) -> p t m", t=PACK),
+                w_raw[i][:].bitcast(U16).rearrange("p (m t) -> p t m", t=PACK),
+            )
+
+        def deal_scales(plane, rows):
+            nc.vector.tensor_copy(
+                plane[:].rearrange("p (i t m) -> p i t m", m=P, t=PACK),
+                rows[:].rearrange("p (i m t) -> p i t m", m=P, t=PACK),
+            )
+
+        for i in range(3):
+            deal_words(i)
+        w12_plane = sb.tile([P, 2 * H], U8, name="w12_plane", align_bytes=64)
+        w3_plane = sb.tile([P, N], U8, name="w3_plane", align_bytes=64)
+        w_planes = (w12_plane[:, :H], w12_plane[:, H:], w3_plane[:])
+        deal_scales(w12_plane, w12_scale_rows)
+
+        picked_words = [sb.tile([P, S], U32, name="picked_words%d" % i, align_bytes=64) for i in range(2)]
+        nc.vector.tensor_copy(picked_words[0][:], x_table[:].bitcast(U32).indirect(offs_t[:]))
+        nc.vector.tensor_copy(picked_words[1][:], x_table[:].bitcast(U32).indirect(hz_t[:]))
+        deal_scales(w3_plane, w3_scale_rows)
+
+        def product(out, i, t, codes, plane):
+            nc.tensor.matmul_mx(
+                out=out,
+                lhsT=w_codes[i][:, 2 * P * t : 2 * P * (t + 1)].bitcast(FP4X4),
+                lhsT_scale=w_planes[i][:, P * t : P * (t + 1)],
+                rhs=codes.bitcast(FP8X4),
+                rhs_scale=plane,
+                start=True,
+                stop=True,
+            )
+
+        first = sb.tile([P, PACK, S], F32, name="first")
+        second = sb.tile([P, PACK, S], F32, name="second")
+        for t in range(PACK):
+            y_ps = ps.tile([P, S], F32, name="y_ps", tag="a%d" % t)
+            d_ps = ps.tile([P, S], F32, name="d_ps", tag="b%d" % t)
+            product(y_ps[:], 0, t, picked_words[0][:], picked_plane[:, :S])
+            product(d_ps[:], 1, t, picked_words[1][:], picked_plane[:, S:])
+            y_sb = sb.tile([P, 2 * S], F32, name="y_sb%d" % t)
+            d_sb = sb.tile([P, 2 * S], F32, name="d_sb%d" % t)
+            y_n1 = sb.tile([P, S], F32, name="y_n1%d" % t)
+            nc.scalar.activation(y_sb[:, :S], y_ps[:], COPY, scale=gain[:, t : t + 1])
+            if t == 0:
+                nc.vector.tensor_copy(d_sb[:, :S], d_ps[:])
+            else:
+                nc.scalar.copy(d_sb[:, :S], d_ps[:])
+            nc.scalar.activation(y_n1[:], y_sb[:].indirect(n1_t[:]), COPY)
+            nc.vector.tensor_tensor(first[:, t, :], d_sb[:].indirect(n2_t[:]), y_sb[:, :S], MULT)
+            nc.vector.tensor_tensor(second[:, t, :], y_n1[:], d_sb[:, :S], MULT)
+
+        h_last = []
+        h_sb = [sb.tile([P, S], F32, name="h_sb%d" % t) for t in range(PACK)]
+        z16 = [sb.tile([P, HALF, PACK], BF16, name="z16_%d" % c, align_bytes=64) for c in range(2)]
+        for c in range(2):
+            cols = slice(c * HALF, (c + 1) * HALF)
+            nc.vector.tensor_tensor(
+                z16[c][:].rearrange("p (c i) t -> p c t i", i=4),
+                first[:, :, cols].rearrange("p t (c i) -> p c t i", i=4),
+                second[:, :, cols].rearrange("p t (c i) -> p c t i", i=4),
+                SUB,
+            )
+        for c in range(2):
+            cols = slice(c * HALF, (c + 1) * HALF)
+            z_codes = sb.tile([P, HALF], U32, name="z_codes%d" % c, align_bytes=64)
+            z_plane = sb.tile([P, HALF], U8, name="z_plane%d" % c, align_bytes=64)
+            nc.vector.quantize_mx(z_codes[:].bitcast(FP8X4), z_plane[:], z16[c][:].rearrange("p c t -> p (c t)"))
+            for t in range(PACK):
+                h_ps = ps.tile([P, HALF], F32, name="h_ps", tag="%s%d" % ("ab"[c], t))
+                product(h_ps[:], 2, t, z_codes[:], z_plane[:])
+                if c == 0:
+                    nc.scalar.copy(h_sb[t][:, cols], h_ps[:])
+                else:
+                    h_last.append(h_ps)
+
+        out_rows = out_0.rearrange("(p t) j -> p t j", t=PACK)
+        res = [sb.tile([P, S], F32, name="res%d" % t) for t in range(PACK)]
+        for pair in ((0, 1), (2, 3)):
+            pa, minus_pb = {}, {}
+            for t in pair:
+                pa[t] = sb.tile([P, W], F32, name="pa%d" % t)
+                minus_pb[t] = sb.tile([P, W], F32, name="minus_pb%d" % t)
+                nc.scalar.copy(h_sb[t][:, HALF:], h_last[t][:])
+                nc.scalar.activation(pa[t][:], h_sb[t][:].indirect(n3_t[:]), COPY)
+                if t == 0:
+                    nc.vector.tensor_scalar(minus_pb[t][:], h_sb[t][:].indirect(n4_t[:]), -1.0, 0.0, MULT, ADD)
+                else:
+                    nc.scalar.activation(minus_pb[t][:], h_sb[t][:].indirect(n4_t[:]), COPY, scale=-1.0)
+                nc.vector.tensor_tensor(res[t][:].indirect(n4_t[:]), pa[t][:], minus_pb[t][:], ADD)
+            for t in pair:
+                pa34 = sb.tile([P, W], F32, name="pa34_%d" % t)
+                pb34 = sb.tile([P, W], F32, name="pb34_%d" % t)
+                nc.scalar.activation(pa34[:], pa[t][:], COPY, scale=0.75)
+                nc.scalar.activation(pb34[:], minus_pb[t][:], COPY, scale=-0.75)
+                nc.vector.tensor_tensor(res[t][:].indirect(n3_t[:]), pa34[:], pb34[:], ADD)
+                nc.sync.dma_start(out_rows[:, t, :], res[t][:])
+
+        out16 = [sb.tile([P, PACK, HALF], BF16, name="out16_%d" % c, align_bytes=64) for c in range(2)]
+        woven = [sb.tile([P, HALF, PACK], BF16, name="woven%d" % c, align_bytes=64) for c in range(2)]
+        for t in range(PACK - 1):
+            for c in range(2):
+                nc.scalar.copy(out16[c][:, t, :], res[t][:, c * HALF : (c + 1) * HALF])
+        copies = (nc.vector.tensor_copy, nc.scalar.copy)
+        for c in range(2):
+            copies[c](out16[c][:, PACK - 1, :], res[PACK - 1][:, c * HALF : (c + 1) * HALF])
+            copies[c](
+                woven[c][:].rearrange("p (c i) t -> p c t i", i=4),
+                out16[c][:].rearrange("p t (c i) -> p c t i", i=4),
+            )
+        out_plane = sb.tile([P, S], U8, name="out_plane", align_bytes=64)
+        out_words = out_1[0].rearrange("p n t -> p (n t)").bitcast(I32)
+        for c in range(2):
+            cols = slice(c * HALF, (c + 1) * HALF)
+            out_codes = sb.tile([P, HALF], I32, name="out_codes%d" % c, align_bytes=64)
+            nc.vector.quantize_mx(out_codes[:].bitcast(FP8X4), out_plane[:, cols], woven[c][:].rearrange("p c t -> p (c t)"))
+            nc.sync.dma_start(out_words[:, cols], out_codes[:])
+        for q in range(4):
+            nc.scalar.dma_start(out_2[0, 4 * q : 4 * q + 4, :].bitcast(I32), out_plane[32 * q : 32 * q + 4, :].bitcast(I32))

@@ -40,43 +40,35 @@ def tile_picked_twhcrossbhaar_none_po_kernel(
 
         x_scale_rows = sb.tile([P, T], U8, name="x_scale_rows", align_bytes=64)
         nc.gpsimd.memset(x_scale_rows[:].bitcast(I32), 0)
-        nc.sync.dma_start(x_scale_rows[0:P:8, :].bitcast(I32), x_scales[0].bitcast(I32))
+        nc.scalar.dma_start(x_scale_rows[0:P:8, :].bitcast(I32), x_scales[0].bitcast(I32))
         hz_t = load_list("hz_t", hz)
         offs_t = load_list("offs_t", offs)
-        n1_t = load_list("n1_t", n1)
-        n2_t = load_list("n2_t", n2)
-        n3_t = load_list("n3_t", n3)
-        n4_t = load_list("n4_t", n4)
+        w_words = (w1_words, w2_words, w3_words)
+        w_raw = [sb.tile([P, 2 * H], U8, name="w_raw%d" % i, tag="w_raw%d" % (i % 2), align_bytes=64) for i in range(2)]
+        w_scale_in = sb.tile([16, 2 * H], U8, name="w_scale_in", align_bytes=64)
+        nc.scalar.dma_start(w_scale_in[:, :H].bitcast(I32), w1_scales[0].bitcast(I32))
+        nc.scalar.dma_start(w_scale_in[:, H:].bitcast(I32), w2_scales[0].bitcast(I32))
         x_table = sb.tile([P, T], I32, name="x_table", align_bytes=64)
         nc.sync.dma_start(x_table[:], x_words[0].rearrange("p n t -> p (n t)").bitcast(I32))
+        nc.scalar.dma_start(w_raw[0][:].bitcast(I32), w_words[0][0].bitcast(I32))
+        nc.sync.dma_start(w_raw[1][:].bitcast(I32), w_words[1][0].bitcast(I32))
+        w_scale_rows = sb.tile([P, 2 * H], U8, name="w_scale_rows", align_bytes=64)
+        nc.vector.memset(w_scale_rows[:].bitcast(I32), 0)
+        for q in range(4):
+            nc.sync.dma_start(w_scale_rows[32 * q : 32 * q + 4, :].bitcast(I32), w_scale_in[4 * q : 4 * q + 4, :].bitcast(I32))
 
-        w_words = (w1_words, w2_words, w3_words)
-        w_raw = [sb.tile([P, 2 * H], U8, name="w_raw%d" % i, align_bytes=64) for i in range(3)]
-        w12_scale_rows = sb.tile([P, 2 * H], U8, name="w12_scale_rows", align_bytes=64)
-        nc.vector.memset(w12_scale_rows[:].bitcast(I32), 0)
         picked_plane = sb.tile([P, 2 * S], U8, name="picked_plane", align_bytes=64)
-        nc.vector.memset(picked_plane[:].bitcast(I32), 0)
-        w3_scale_rows = sb.tile([P, N], U8, name="w3_scale_rows", align_bytes=64)
-        nc.vector.memset(w3_scale_rows[:].bitcast(I32), 0)
-
-        def load_scale_rows(queue, rows, scales):
-            for q in range(4):
-                queue.dma_start(rows[32 * q : 32 * q + 4, :].bitcast(I32), scales[0, 4 * q : 4 * q + 4, :].bitcast(I32))
-
-        load_scale_rows(nc.sync, w12_scale_rows[:, :H], w1_scales)
-        load_scale_rows(nc.sync, w12_scale_rows[:, H:], w2_scales)
-        gain_in = sb.tile([P, PACK], F32, name="gain_in")
-        for i in range(2):
-            nc.gpsimd.dma_start(w_raw[i][:].bitcast(I32), w_words[i][0].bitcast(I32))
-        nc.gpsimd.dma_start(gain_in[:], gn.rearrange("(p t) o -> p (t o)", t=PACK))
-        nc.gpsimd.dma_start(w_raw[2][:].bitcast(I32), w_words[2][0].bitcast(I32))
-
         picked_bytes = sb.tile([P, 2 * S], U8, name="picked_bytes", align_bytes=64)
         nc.vector.tensor_copy(picked_bytes[:, S:], x_scale_rows[:].indirect(hz_t[:]))
         nc.vector.tensor_copy(picked_bytes[:, :S], x_scale_rows[:].indirect(offs_t[:]))
         for b in range(4):
             nc.sync.dma_start(picked_plane[b:P:32, :].bitcast(I32), picked_bytes[8 * b : P : 32, :].bitcast(I32))
-        load_scale_rows(nc.gpsimd, w3_scale_rows[:], w3_scales)
+        n1_t = load_list("n1_t", n1)
+        n2_t = load_list("n2_t", n2)
+        gain_in = sb.tile([P, PACK], F32, name="gain_in")
+        nc.gpsimd.dma_start(gain_in[:], gn.rearrange("(p t) o -> p (t o)", t=PACK))
+        n3_t = load_list("n3_t", n3)
+        n4_t = load_list("n4_t", n4)
         gain = sb.tile([P, PACK], F32, name="gain")
         nc.scalar.activation(gain[:], gain_in[:], COPY, scale=0.75)
 
@@ -91,20 +83,24 @@ def tile_picked_twhcrossbhaar_none_po_kernel(
         def deal_scales(plane, rows):
             nc.vector.tensor_copy(
                 plane[:].rearrange("p (i t m) -> p i t m", m=P, t=PACK),
-                rows[:].rearrange("p (i m t) -> p i t m", m=P, t=PACK),
+                rows.rearrange("p (i m t) -> p i t m", m=P, t=PACK),
             )
 
-        for i in range(3):
+        for i in range(2):
             deal_words(i)
         w12_plane = sb.tile([P, 2 * H], U8, name="w12_plane", align_bytes=64)
         w3_plane = sb.tile([P, N], U8, name="w3_plane", align_bytes=64)
         w_planes = (w12_plane[:, :H], w12_plane[:, H:], w3_plane[:])
-        deal_scales(w12_plane, w12_scale_rows)
+        deal_scales(w12_plane, w_scale_rows[:])
 
         picked_words = [sb.tile([P, S], U32, name="picked_words%d" % i, align_bytes=64) for i in range(2)]
         nc.vector.tensor_copy(picked_words[0][:], x_table[:].bitcast(U32).indirect(offs_t[:]))
         nc.vector.tensor_copy(picked_words[1][:], x_table[:].bitcast(U32).indirect(hz_t[:]))
-        deal_scales(w3_plane, w3_scale_rows)
+        w3_raw = sb.tile([P, 2 * N], U8, name="w3_raw", tag="w_raw0", align_bytes=64)
+        w_raw.append(w3_raw)
+        nc.sync.dma_start(w3_raw[:].bitcast(I32), w3_words[0].bitcast(I32))
+        for q in range(4):
+            nc.sync.dma_start(w_scale_rows[32 * q : 32 * q + 4, :N].bitcast(I32), w3_scales[0, 4 * q : 4 * q + 4, :].bitcast(I32))
 
         def product(out, i, t, codes, plane):
             nc.tensor.matmul_mx(
@@ -119,22 +115,36 @@ def tile_picked_twhcrossbhaar_none_po_kernel(
 
         first = sb.tile([P, PACK, S], F32, name="first")
         second = sb.tile([P, PACK, S], F32, name="second")
-        for t in range(PACK):
+        y_sb = [sb.tile([P, 2 * S], F32, name="y_sb%d" % t) for t in range(PACK)]
+        d_sb = [sb.tile([P, 2 * S], F32, name="d_sb%d" % t) for t in range(PACK)]
+
+        def project(t):
             y_ps = ps.tile([P, S], F32, name="y_ps", tag="a%d" % t)
             d_ps = ps.tile([P, S], F32, name="d_ps", tag="b%d" % t)
             product(y_ps[:], 0, t, picked_words[0][:], picked_plane[:, :S])
             product(d_ps[:], 1, t, picked_words[1][:], picked_plane[:, S:])
-            y_sb = sb.tile([P, 2 * S], F32, name="y_sb%d" % t)
-            d_sb = sb.tile([P, 2 * S], F32, name="d_sb%d" % t)
-            y_n1 = sb.tile([P, S], F32, name="y_n1%d" % t)
-            nc.scalar.activation(y_sb[:, :S], y_ps[:], COPY, scale=gain[:, t : t + 1])
+            nc.scalar.activation(y_sb[t][:, :S], y_ps[:], COPY, scale=gain[:, t : t + 1])
             if t == 0:
-                nc.vector.tensor_copy(d_sb[:, :S], d_ps[:])
+                nc.vector.tensor_copy(d_sb[t][:, :S], d_ps[:])
             else:
-                nc.scalar.copy(d_sb[:, :S], d_ps[:])
-            nc.scalar.activation(y_n1[:], y_sb[:].indirect(n1_t[:]), COPY)
-            nc.vector.tensor_tensor(first[:, t, :], d_sb[:].indirect(n2_t[:]), y_sb[:, :S], MULT)
-            nc.vector.tensor_tensor(second[:, t, :], y_n1[:], d_sb[:, :S], MULT)
+                nc.scalar.copy(d_sb[t][:, :S], d_ps[:])
+            nc.vector.tensor_tensor(first[:, t, :], d_sb[t][:].indirect(n2_t[:]), y_sb[t][:, :S], MULT)
+
+        def second_by_scalar_gather(t):
+            y_n1 = sb.tile([P, S], F32, name="y_n1%d" % t)
+            nc.scalar.activation(y_n1[:], y_sb[t][:].indirect(n1_t[:]), COPY)
+            nc.vector.tensor_tensor(second[:, t, :], y_n1[:], d_sb[t][:, :S], MULT)
+
+        project(0)
+        project(1)
+        project(2)
+        second_by_scalar_gather(0)
+        project(3)
+        second_by_scalar_gather(1)
+        nc.vector.tensor_tensor(second[:, 3, :], y_sb[3][:].indirect(n1_t[:]), d_sb[3][:, :S], MULT)
+        second_by_scalar_gather(2)
+        deal_words(2)
+        deal_scales(w3_plane, w_scale_rows[:, :N])
 
         h_last = []
         h_sb = [sb.tile([P, S], F32, name="h_sb%d" % t) for t in range(PACK)]

@@ -38,21 +38,22 @@ def tile_picked_twhcrossbhaar_none_po_kernel(
             nc.sync.dma_start(tile[:], src)
             return tile
 
-        x_scale_rows = sb.tile([P, T], U8, name="x_scale_rows", align_bytes=64)
+        x_scale_rows = sb.tile([P, T], U8, name="x_scale_rows", tag="early", align_bytes=64)
         nc.gpsimd.memset(x_scale_rows[:].bitcast(I32), 0)
         nc.scalar.dma_start(x_scale_rows[0:P:8, :].bitcast(I32), x_scales[0].bitcast(I32))
         hz_t = load_list("hz_t", hz)
         offs_t = load_list("offs_t", offs)
         w_words = (w1_words, w2_words, w3_words)
-        w_raw = [sb.tile([P, 2 * H], U8, name="w_raw%d" % i, tag="w_raw%d" % (i % 2), align_bytes=64) for i in range(2)]
-        w_scale_in = sb.tile([16, 2 * H], U8, name="w_scale_in", align_bytes=64)
+        w_raw = [sb.tile([P, 2 * H], U8, name="w_raw%d" % i, align_bytes=64) for i in range(2)]
+        w_scale_in = sb.tile([16, 3 * H], U8, name="w_scale_in", tag="staged", align_bytes=64)
         nc.scalar.dma_start(w_scale_in[:, :H].bitcast(I32), w1_scales[0].bitcast(I32))
-        nc.scalar.dma_start(w_scale_in[:, H:].bitcast(I32), w2_scales[0].bitcast(I32))
+        nc.scalar.dma_start(w_scale_in[:, H : 2 * H].bitcast(I32), w2_scales[0].bitcast(I32))
+        nc.gpsimd.dma_start(w_scale_in[:, 2 * H :].bitcast(I32), w3_scales[0].bitcast(I32))
         x_table = sb.tile([P, T], I32, name="x_table", align_bytes=64)
         nc.sync.dma_start(x_table[:], x_words[0].rearrange("p n t -> p (n t)").bitcast(I32))
         nc.scalar.dma_start(w_raw[0][:].bitcast(I32), w_words[0][0].bitcast(I32))
         nc.sync.dma_start(w_raw[1][:].bitcast(I32), w_words[1][0].bitcast(I32))
-        w_scale_rows = sb.tile([P, 2 * H], U8, name="w_scale_rows", align_bytes=64)
+        w_scale_rows = sb.tile([P, 3 * H], U8, name="w_scale_rows", align_bytes=64)
         nc.vector.memset(w_scale_rows[:].bitcast(I32), 0)
         for q in range(4):
             nc.sync.dma_start(w_scale_rows[32 * q : 32 * q + 4, :].bitcast(I32), w_scale_in[4 * q : 4 * q + 4, :].bitcast(I32))
@@ -91,16 +92,18 @@ def tile_picked_twhcrossbhaar_none_po_kernel(
         w12_plane = sb.tile([P, 2 * H], U8, name="w12_plane", align_bytes=64)
         w3_plane = sb.tile([P, N], U8, name="w3_plane", align_bytes=64)
         w_planes = (w12_plane[:, :H], w12_plane[:, H:], w3_plane[:])
-        deal_scales(w12_plane, w_scale_rows[:])
+        deal_scales(w12_plane, w_scale_rows[:, : 2 * H])
 
-        picked_words = [sb.tile([P, S], U32, name="picked_words%d" % i, align_bytes=64) for i in range(2)]
+        picked_words = [
+            sb.tile([P, S], U32, name="words_by_offs", align_bytes=64),
+            sb.tile([P, S], U32, name="words_by_hz", tag="staged", align_bytes=64),
+        ]
         nc.vector.tensor_copy(picked_words[0][:], x_table[:].bitcast(U32).indirect(offs_t[:]))
         nc.vector.tensor_copy(picked_words[1][:], x_table[:].bitcast(U32).indirect(hz_t[:]))
-        w3_raw = sb.tile([P, 2 * N], U8, name="w3_raw", tag="w_raw0", align_bytes=64)
+        w3_raw = sb.tile([P, 2 * N], U8, name="w3_raw", tag="early", align_bytes=64)
         w_raw.append(w3_raw)
         nc.sync.dma_start(w3_raw[:].bitcast(I32), w3_words[0].bitcast(I32))
-        for q in range(4):
-            nc.sync.dma_start(w_scale_rows[32 * q : 32 * q + 4, :N].bitcast(I32), w3_scales[0, 4 * q : 4 * q + 4, :].bitcast(I32))
+        deal_scales(w3_plane, w_scale_rows[:, 2 * H :])
 
         def product(out, i, t, codes, plane):
             nc.tensor.matmul_mx(
@@ -130,45 +133,46 @@ def tile_picked_twhcrossbhaar_none_po_kernel(
                 nc.scalar.copy(d_sb[t][:, :S], d_ps[:])
             nc.vector.tensor_tensor(first[:, t, :], d_sb[t][:].indirect(n2_t[:]), y_sb[t][:, :S], MULT)
 
-        def second_by_scalar_gather(t):
+        z_rows = sb.tile([P, PACK, S], BF16, name="z_rows", align_bytes=64)
+
+        def cross(t):
             y_n1 = sb.tile([P, S], F32, name="y_n1%d" % t)
             nc.scalar.activation(y_n1[:], y_sb[t][:].indirect(n1_t[:]), COPY)
             nc.vector.tensor_tensor(second[:, t, :], y_n1[:], d_sb[t][:, :S], MULT)
 
+        def round_z(t, cols):
+            nc.vector.tensor_tensor(z_rows[:, t, cols], first[:, t, cols], second[:, t, cols], SUB)
+
         project(0)
         project(1)
         project(2)
-        second_by_scalar_gather(0)
+        cross(0)
         project(3)
-        second_by_scalar_gather(1)
-        nc.vector.tensor_tensor(second[:, 3, :], y_sb[3][:].indirect(n1_t[:]), d_sb[3][:, :S], MULT)
-        second_by_scalar_gather(2)
+        round_z(0, slice(0, S))
+        for t in range(1, PACK):
+            cross(t)
+            if t < PACK - 1:
+                round_z(t, slice(0, S))
         deal_words(2)
-        deal_scales(w3_plane, w_scale_rows[:, :N])
 
-        h_last = []
         h_sb = [sb.tile([P, S], F32, name="h_sb%d" % t) for t in range(PACK)]
         z16 = [sb.tile([P, HALF, PACK], BF16, name="z16_%d" % c, align_bytes=64) for c in range(2)]
-        for c in range(2):
+        copies = (nc.vector.tensor_copy, nc.scalar.copy)
+        for c in (1, 0):
             cols = slice(c * HALF, (c + 1) * HALF)
-            nc.vector.tensor_tensor(
+            round_z(PACK - 1, cols)
+            copies[c](
                 z16[c][:].rearrange("p (c i) t -> p c t i", i=4),
-                first[:, :, cols].rearrange("p t (c i) -> p c t i", i=4),
-                second[:, :, cols].rearrange("p t (c i) -> p c t i", i=4),
-                SUB,
+                z_rows[:, :, cols].rearrange("p t (c i) -> p c t i", i=4),
             )
+        z_codes = [sb.tile([P, HALF], U32, name="z_codes%d" % c, align_bytes=64) for c in range(2)]
+        z_plane = [sb.tile([P, HALF], U8, name="z_plane%d" % c, align_bytes=64) for c in range(2)]
         for c in range(2):
-            cols = slice(c * HALF, (c + 1) * HALF)
-            z_codes = sb.tile([P, HALF], U32, name="z_codes%d" % c, align_bytes=64)
-            z_plane = sb.tile([P, HALF], U8, name="z_plane%d" % c, align_bytes=64)
-            nc.vector.quantize_mx(z_codes[:].bitcast(FP8X4), z_plane[:], z16[c][:].rearrange("p c t -> p (c t)"))
-            for t in range(PACK):
-                h_ps = ps.tile([P, HALF], F32, name="h_ps", tag="%s%d" % ("ab"[c], t))
-                product(h_ps[:], 2, t, z_codes[:], z_plane[:])
-                if c == 0:
-                    nc.scalar.copy(h_sb[t][:, cols], h_ps[:])
-                else:
-                    h_last.append(h_ps)
+            nc.vector.quantize_mx(z_codes[c][:].bitcast(FP8X4), z_plane[c][:], z16[c][:].rearrange("p c t -> p (c t)"))
+        h_ps = [[ps.tile([P, HALF], F32, name="h_ps", tag="%s%d" % ("ab"[c], t)) for c in range(2)] for t in range(PACK)]
+        for t in range(PACK):
+            for c in range(2):
+                product(h_ps[t][c][:], 2, t, z_codes[c][:], z_plane[c][:])
 
         out_rows = out_0.rearrange("(p t) j -> p t j", t=PACK)
         res = [sb.tile([P, S], F32, name="res%d" % t) for t in range(PACK)]
@@ -177,7 +181,11 @@ def tile_picked_twhcrossbhaar_none_po_kernel(
             for t in pair:
                 pa[t] = sb.tile([P, W], F32, name="pa%d" % t)
                 minus_pb[t] = sb.tile([P, W], F32, name="minus_pb%d" % t)
-                nc.scalar.copy(h_sb[t][:, HALF:], h_last[t][:])
+                nc.scalar.copy(h_sb[t][:, :HALF], h_ps[t][0][:])
+                if t == 0:
+                    nc.vector.tensor_copy(h_sb[t][:, HALF:], h_ps[t][1][:])
+                else:
+                    nc.scalar.copy(h_sb[t][:, HALF:], h_ps[t][1][:])
                 nc.scalar.activation(pa[t][:], h_sb[t][:].indirect(n3_t[:]), COPY)
                 if t == 0:
                     nc.vector.tensor_scalar(minus_pb[t][:], h_sb[t][:].indirect(n4_t[:]), -1.0, 0.0, MULT, ADD)
@@ -192,17 +200,16 @@ def tile_picked_twhcrossbhaar_none_po_kernel(
                 nc.vector.tensor_tensor(res[t][:].indirect(n3_t[:]), pa34[:], pb34[:], ADD)
                 nc.sync.dma_start(out_rows[:, t, :], res[t][:])
 
-        out16 = [sb.tile([P, PACK, HALF], BF16, name="out16_%d" % c, align_bytes=64) for c in range(2)]
+        out16 = sb.tile([P, PACK, S], BF16, name="out16", align_bytes=64)
         woven = [sb.tile([P, HALF, PACK], BF16, name="woven%d" % c, align_bytes=64) for c in range(2)]
         for t in range(PACK - 1):
-            for c in range(2):
-                nc.scalar.copy(out16[c][:, t, :], res[t][:, c * HALF : (c + 1) * HALF])
-        copies = (nc.vector.tensor_copy, nc.scalar.copy)
+            nc.scalar.copy(out16[:, t, :], res[t][:])
         for c in range(2):
-            copies[c](out16[c][:, PACK - 1, :], res[PACK - 1][:, c * HALF : (c + 1) * HALF])
+            cols = slice(c * HALF, (c + 1) * HALF)
+            copies[c](out16[:, PACK - 1, cols], res[PACK - 1][:, cols])
             copies[c](
                 woven[c][:].rearrange("p (c i) t -> p c t i", i=4),
-                out16[c][:].rearrange("p t (c i) -> p c t i", i=4),
+                out16[:, :, cols].rearrange("p t (c i) -> p c t i", i=4),
             )
         out_plane = sb.tile([P, S], U8, name="out_plane", align_bytes=64)
         out_words = out_1[0].rearrange("p n t -> p (n t)").bitcast(I32)

@@ -2,7 +2,7 @@ from contextlib import ExitStack
 
 import concourse.mybir as mybir
 
-K, T, S, N, H, W = 512, 2048, 512, 512, 512, 256
+T, S, N, H, W = 2048, 512, 512, 512, 256
 FLOPS = 3 * 2 * 512 * 512 * 512
 
 F32 = mybir.dt.float32
@@ -21,6 +21,9 @@ SUB = mybir.AluOpType.subtract
 P = 128
 PACK = 4
 HALF = S // 2
+X_FIRST = 768
+OUT_VECTOR = 384
+H_BANKS = (("y0", "d0"), ("y1", "d1"), ("y0", "d2"), ("d0", "d3"))
 
 
 def tile_picked_twhcrossbhaar_none_po_kernel(
@@ -40,19 +43,20 @@ def tile_picked_twhcrossbhaar_none_po_kernel(
 
         x_scale_rows = sb.tile([P, T], U8, name="x_scale_rows", tag="early", align_bytes=64)
         nc.gpsimd.memset(x_scale_rows[:].bitcast(I32), 0)
-        nc.scalar.dma_start(x_scale_rows[0:P:8, :].bitcast(I32), x_scales[0].bitcast(I32))
+        nc.sync.dma_start(x_scale_rows[0:P:8, :].bitcast(I32), x_scales[0].bitcast(I32))
         hz_t = load_list("hz_t", hz)
         offs_t = load_list("offs_t", offs)
-        w_words = (w1_words, w2_words, w3_words)
         w_raw = [sb.tile([P, 2 * H], U8, name="w_raw%d" % i, align_bytes=64) for i in range(2)]
         w_scale_in = sb.tile([16, 3 * H], U8, name="w_scale_in", tag="staged", align_bytes=64)
         nc.scalar.dma_start(w_scale_in[:, :H].bitcast(I32), w1_scales[0].bitcast(I32))
         nc.scalar.dma_start(w_scale_in[:, H : 2 * H].bitcast(I32), w2_scales[0].bitcast(I32))
         nc.gpsimd.dma_start(w_scale_in[:, 2 * H :].bitcast(I32), w3_scales[0].bitcast(I32))
+        nc.sync.dma_start(w_raw[0][:].bitcast(I32), w1_words[0].bitcast(I32))
         x_table = sb.tile([P, T], I32, name="x_table", align_bytes=64)
-        nc.sync.dma_start(x_table[:], x_words[0].rearrange("p n t -> p (n t)").bitcast(I32))
-        nc.scalar.dma_start(w_raw[0][:].bitcast(I32), w_words[0][0].bitcast(I32))
-        nc.sync.dma_start(w_raw[1][:].bitcast(I32), w_words[1][0].bitcast(I32))
+        x_columns = x_words[0].rearrange("p n t -> p (n t)").bitcast(I32)
+        nc.sync.dma_start(x_table[:, :X_FIRST], x_columns[:, :X_FIRST])
+        nc.sync.dma_start(x_table[:, X_FIRST:], x_columns[:, X_FIRST:])
+        nc.sync.dma_start(w_raw[1][:].bitcast(I32), w2_words[0].bitcast(I32))
         w_scale_rows = sb.tile([P, 3 * H], U8, name="w_scale_rows", align_bytes=64)
         nc.vector.memset(w_scale_rows[:].bitcast(I32), 0)
         for q in range(4):
@@ -94,12 +98,10 @@ def tile_picked_twhcrossbhaar_none_po_kernel(
         w_planes = (w12_plane[:, :H], w12_plane[:, H:], w3_plane[:])
         deal_scales(w12_plane, w_scale_rows[:, : 2 * H])
 
-        picked_words = [
-            sb.tile([P, S], U32, name="words_by_offs", align_bytes=64),
-            sb.tile([P, S], U32, name="words_by_hz", tag="staged", align_bytes=64),
-        ]
-        nc.vector.tensor_copy(picked_words[0][:], x_table[:].bitcast(U32).indirect(offs_t[:]))
-        nc.vector.tensor_copy(picked_words[1][:], x_table[:].bitcast(U32).indirect(hz_t[:]))
+        words_by_offs = sb.tile([P, S], U32, name="words_by_offs", align_bytes=64)
+        words_by_hz = sb.tile([P, S], U32, name="words_by_hz", tag="staged", align_bytes=64)
+        nc.vector.tensor_copy(words_by_offs[:], x_table[:].bitcast(U32).indirect(offs_t[:]))
+        nc.vector.tensor_copy(words_by_hz[:], x_table[:].bitcast(U32).indirect(hz_t[:]))
         w3_raw = sb.tile([P, 2 * N], U8, name="w3_raw", tag="early", align_bytes=64)
         w_raw.append(w3_raw)
         nc.sync.dma_start(w3_raw[:].bitcast(I32), w3_words[0].bitcast(I32))
@@ -116,63 +118,40 @@ def tile_picked_twhcrossbhaar_none_po_kernel(
                 stop=True,
             )
 
-        first = sb.tile([P, PACK, S], F32, name="first")
-        second = sb.tile([P, PACK, S], F32, name="second")
+        y_d_n2 = sb.tile([P, PACK, S], F32, name="y_d_n2")
+        y_n1_d = sb.tile([P, PACK, S], F32, name="y_n1_d")
         y_sb = [sb.tile([P, 2 * S], F32, name="y_sb%d" % t) for t in range(PACK)]
         d_sb = [sb.tile([P, 2 * S], F32, name="d_sb%d" % t) for t in range(PACK)]
-
-        def project(t):
-            y_ps = ps.tile([P, S], F32, name="y_ps", tag="a%d" % t)
-            d_ps = ps.tile([P, S], F32, name="d_ps", tag="b%d" % t)
-            product(y_ps[:], 0, t, picked_words[0][:], picked_plane[:, :S])
-            product(d_ps[:], 1, t, picked_words[1][:], picked_plane[:, S:])
+        for t in range(PACK):
+            y_ps = ps.tile([P, S], F32, name="y_ps", tag="y%d" % t)
+            d_ps = ps.tile([P, S], F32, name="d_ps", tag="d%d" % t)
+            product(y_ps[:], 0, t, words_by_offs[:], picked_plane[:, :S])
+            product(d_ps[:], 1, t, words_by_hz[:], picked_plane[:, S:])
+            y_n1 = sb.tile([P, S], F32, name="y_n1%d" % t)
             nc.scalar.activation(y_sb[t][:, :S], y_ps[:], COPY, scale=gain[:, t : t + 1])
             if t == 0:
                 nc.vector.tensor_copy(d_sb[t][:, :S], d_ps[:])
             else:
                 nc.scalar.copy(d_sb[t][:, :S], d_ps[:])
-            nc.vector.tensor_tensor(first[:, t, :], d_sb[t][:].indirect(n2_t[:]), y_sb[t][:, :S], MULT)
-
-        z_rows = sb.tile([P, PACK, S], BF16, name="z_rows", align_bytes=64)
-
-        def cross(t):
-            y_n1 = sb.tile([P, S], F32, name="y_n1%d" % t)
             nc.scalar.activation(y_n1[:], y_sb[t][:].indirect(n1_t[:]), COPY)
-            nc.vector.tensor_tensor(second[:, t, :], y_n1[:], d_sb[t][:, :S], MULT)
-
-        def round_z(t, cols):
-            nc.vector.tensor_tensor(z_rows[:, t, cols], first[:, t, cols], second[:, t, cols], SUB)
-
-        project(0)
-        project(1)
-        project(2)
-        cross(0)
-        project(3)
-        round_z(0, slice(0, S))
-        for t in range(1, PACK):
-            cross(t)
-            if t < PACK - 1:
-                round_z(t, slice(0, S))
+            nc.vector.tensor_tensor(y_d_n2[:, t, :], d_sb[t][:].indirect(n2_t[:]), y_sb[t][:, :S], MULT)
+            nc.vector.tensor_tensor(y_n1_d[:, t, :], y_n1[:], d_sb[t][:, :S], MULT)
         deal_words(2)
 
         h_sb = [sb.tile([P, S], F32, name="h_sb%d" % t) for t in range(PACK)]
         z16 = [sb.tile([P, HALF, PACK], BF16, name="z16_%d" % c, align_bytes=64) for c in range(2)]
-        copies = (nc.vector.tensor_copy, nc.scalar.copy)
-        for c in (1, 0):
+        for c in range(2):
             cols = slice(c * HALF, (c + 1) * HALF)
-            round_z(PACK - 1, cols)
-            copies[c](
+            nc.vector.tensor_tensor(
                 z16[c][:].rearrange("p (c i) t -> p c t i", i=4),
-                z_rows[:, :, cols].rearrange("p t (c i) -> p c t i", i=4),
+                y_d_n2[:, :, cols].rearrange("p t (c i) -> p c t i", i=4),
+                y_n1_d[:, :, cols].rearrange("p t (c i) -> p c t i", i=4),
+                SUB,
             )
         z_codes = [sb.tile([P, HALF], U32, name="z_codes%d" % c, align_bytes=64) for c in range(2)]
         z_plane = [sb.tile([P, HALF], U8, name="z_plane%d" % c, align_bytes=64) for c in range(2)]
         for c in range(2):
             nc.vector.quantize_mx(z_codes[c][:].bitcast(FP8X4), z_plane[c][:], z16[c][:].rearrange("p c t -> p (c t)"))
-        h_ps = [[ps.tile([P, HALF], F32, name="h_ps", tag="%s%d" % ("ab"[c], t)) for c in range(2)] for t in range(PACK)]
-        for t in range(PACK):
-            for c in range(2):
-                product(h_ps[t][c][:], 2, t, z_codes[c][:], z_plane[c][:])
 
         out_rows = out_0.rearrange("(p t) j -> p t j", t=PACK)
         res = [sb.tile([P, S], F32, name="res%d" % t) for t in range(PACK)]
@@ -181,11 +160,13 @@ def tile_picked_twhcrossbhaar_none_po_kernel(
             for t in pair:
                 pa[t] = sb.tile([P, W], F32, name="pa%d" % t)
                 minus_pb[t] = sb.tile([P, W], F32, name="minus_pb%d" % t)
-                nc.scalar.copy(h_sb[t][:, :HALF], h_ps[t][0][:])
-                if t == 0:
-                    nc.vector.tensor_copy(h_sb[t][:, HALF:], h_ps[t][1][:])
-                else:
-                    nc.scalar.copy(h_sb[t][:, HALF:], h_ps[t][1][:])
+                for c in range(2):
+                    h_ps = ps.tile([P, HALF], F32, name="h_ps", tag=H_BANKS[t][c])
+                    product(h_ps[:], 2, t, z_codes[c][:], z_plane[c][:])
+                    if (t, c) == (0, 1):
+                        nc.vector.tensor_copy(h_sb[t][:, HALF:], h_ps[:])
+                    else:
+                        nc.scalar.copy(h_sb[t][:, c * HALF : (c + 1) * HALF], h_ps[:])
                 nc.scalar.activation(pa[t][:], h_sb[t][:].indirect(n3_t[:]), COPY)
                 if t == 0:
                     nc.vector.tensor_scalar(minus_pb[t][:], h_sb[t][:].indirect(n4_t[:]), -1.0, 0.0, MULT, ADD)
@@ -201,22 +182,24 @@ def tile_picked_twhcrossbhaar_none_po_kernel(
                 nc.sync.dma_start(out_rows[:, t, :], res[t][:])
 
         out16 = sb.tile([P, PACK, S], BF16, name="out16", align_bytes=64)
-        woven = [sb.tile([P, HALF, PACK], BF16, name="woven%d" % c, align_bytes=64) for c in range(2)]
         for t in range(PACK - 1):
             nc.scalar.copy(out16[:, t, :], res[t][:])
-        for c in range(2):
-            cols = slice(c * HALF, (c + 1) * HALF)
-            copies[c](out16[:, PACK - 1, cols], res[PACK - 1][:, cols])
-            copies[c](
-                woven[c][:].rearrange("p (c i) t -> p c t i", i=4),
+        shares = ((nc.vector.tensor_copy, slice(0, OUT_VECTOR)), (nc.scalar.copy, slice(OUT_VECTOR, S)))
+        woven = []
+        for c, (copy, cols) in enumerate(shares):
+            share = sb.tile([P, cols.stop - cols.start, PACK], BF16, name="woven%d" % c, align_bytes=64)
+            woven.append(share)
+            copy(out16[:, PACK - 1, cols], res[PACK - 1][:, cols])
+            copy(
+                share[:].rearrange("p (c i) t -> p c t i", i=4),
                 out16[:, :, cols].rearrange("p t (c i) -> p c t i", i=4),
             )
         out_plane = sb.tile([P, S], U8, name="out_plane", align_bytes=64)
         out_words = out_1[0].rearrange("p n t -> p (n t)").bitcast(I32)
-        for c in range(2):
-            cols = slice(c * HALF, (c + 1) * HALF)
-            out_codes = sb.tile([P, HALF], I32, name="out_codes%d" % c, align_bytes=64)
+        for c, (copy, cols) in enumerate(shares):
+            out_codes = sb.tile([P, cols.stop - cols.start], I32, name="out_codes%d" % c, align_bytes=64)
             nc.vector.quantize_mx(out_codes[:].bitcast(FP8X4), out_plane[:, cols], woven[c][:].rearrange("p c t -> p (c t)"))
             nc.sync.dma_start(out_words[:, cols], out_codes[:])
         for q in range(4):
-            nc.scalar.dma_start(out_2[0, 4 * q : 4 * q + 4, :].bitcast(I32), out_plane[32 * q : 32 * q + 4, :].bitcast(I32))
+            queue = (nc.scalar, nc.sync)[q % 2]
+            queue.dma_start(out_2[0, 4 * q : 4 * q + 4, :].bitcast(I32), out_plane[32 * q : 32 * q + 4, :].bitcast(I32))

@@ -47,17 +47,16 @@ def tile_picked_twhcrossbhaar_none_po_kernel(
         hz_t = load_list("hz_t", hz)
         offs_t = load_list("offs_t", offs)
         w_raw = [sb.tile([P, 2 * H], U8, name="w_raw%d" % i, align_bytes=64) for i in range(2)]
-        w_scale_in = sb.tile([16, 3 * H], U8, name="w_scale_in", tag="staged", align_bytes=64)
+        w_scale_in = sb.tile([16, 2 * H], U8, name="w_scale_in", tag="staged", align_bytes=64)
         nc.scalar.dma_start(w_scale_in[:, :H].bitcast(I32), w1_scales[0].bitcast(I32))
-        nc.scalar.dma_start(w_scale_in[:, H : 2 * H].bitcast(I32), w2_scales[0].bitcast(I32))
-        nc.gpsimd.dma_start(w_scale_in[:, 2 * H :].bitcast(I32), w3_scales[0].bitcast(I32))
+        nc.scalar.dma_start(w_scale_in[:, H:].bitcast(I32), w2_scales[0].bitcast(I32))
         nc.sync.dma_start(w_raw[0][:].bitcast(I32), w1_words[0].bitcast(I32))
         x_table = sb.tile([P, T], I32, name="x_table", align_bytes=64)
         x_columns = x_words[0].rearrange("p n t -> p (n t)").bitcast(I32)
         nc.sync.dma_start(x_table[:, :X_FIRST], x_columns[:, :X_FIRST])
         nc.sync.dma_start(x_table[:, X_FIRST:], x_columns[:, X_FIRST:])
         nc.sync.dma_start(w_raw[1][:].bitcast(I32), w2_words[0].bitcast(I32))
-        w_scale_rows = sb.tile([P, 3 * H], U8, name="w_scale_rows", align_bytes=64)
+        w_scale_rows = sb.tile([P, 2 * H], U8, name="w_scale_rows", align_bytes=64)
         nc.vector.memset(w_scale_rows[:].bitcast(I32), 0)
         for q in range(4):
             nc.sync.dma_start(w_scale_rows[32 * q : 32 * q + 4, :].bitcast(I32), w_scale_in[4 * q : 4 * q + 4, :].bitcast(I32))
@@ -96,7 +95,7 @@ def tile_picked_twhcrossbhaar_none_po_kernel(
         w12_plane = sb.tile([P, 2 * H], U8, name="w12_plane", align_bytes=64)
         w3_plane = sb.tile([P, N], U8, name="w3_plane", align_bytes=64)
         w_planes = (w12_plane[:, :H], w12_plane[:, H:], w3_plane[:])
-        deal_scales(w12_plane, w_scale_rows[:, : 2 * H])
+        deal_scales(w12_plane, w_scale_rows[:])
 
         words_by_offs = sb.tile([P, S], U32, name="words_by_offs", align_bytes=64)
         words_by_hz = sb.tile([P, S], U32, name="words_by_hz", tag="staged", align_bytes=64)
@@ -105,7 +104,8 @@ def tile_picked_twhcrossbhaar_none_po_kernel(
         w3_raw = sb.tile([P, 2 * N], U8, name="w3_raw", tag="early", align_bytes=64)
         w_raw.append(w3_raw)
         nc.sync.dma_start(w3_raw[:].bitcast(I32), w3_words[0].bitcast(I32))
-        deal_scales(w3_plane, w_scale_rows[:, 2 * H :])
+        for q in range(4):
+            nc.sync.dma_start(w_scale_rows[32 * q : 32 * q + 4, :N].bitcast(I32), w3_scales[0, 4 * q : 4 * q + 4, :].bitcast(I32))
 
         def product(out, i, t, codes, plane):
             nc.tensor.matmul_mx(
@@ -137,6 +137,7 @@ def tile_picked_twhcrossbhaar_none_po_kernel(
             nc.vector.tensor_tensor(y_d_n2[:, t, :], d_sb[t][:].indirect(n2_t[:]), y_sb[t][:, :S], MULT)
             nc.vector.tensor_tensor(y_n1_d[:, t, :], y_n1[:], d_sb[t][:, :S], MULT)
         deal_words(2)
+        deal_scales(w3_plane, w_scale_rows[:, :N])
 
         h_sb = [sb.tile([P, S], F32, name="h_sb%d" % t) for t in range(PACK)]
         z16 = [sb.tile([P, HALF, PACK], BF16, name="z16_%d" % c, align_bytes=64) for c in range(2)]

from contextlib import ExitStack

import concourse.mybir as mybir

T, S, N, H, W = 2048, 512, 512, 512, 256
FLOPS = 3 * 2 * 512 * 512 * 512

F32 = mybir.dt.float32
BF16 = mybir.dt.bfloat16
I32 = mybir.dt.int32
U32 = mybir.dt.uint32
U16 = mybir.dt.uint16
U8 = mybir.dt.uint8
FP8X4 = mybir.dt.float8_e4m3fn_x4
FP4X4 = mybir.dt.float4_e2m1fn_x4
COPY = mybir.ActivationFunctionType.Copy
MULT = mybir.AluOpType.mult
ADD = mybir.AluOpType.add
SUB = mybir.AluOpType.subtract

P = 128
PACK = 4
HALF = S // 2
X_FIRST = 768
OUT_VECTOR = 384
H_BANKS = (("y0", "d0"), ("y1", "d1"), ("y0", "d2"), ("d0", "d3"))


def tile_picked_twhcrossbhaar_none_po_kernel(
    tc, x_words, x_scales, w1_words, w1_scales, w2_words, w2_scales, gn, w3_words, w3_scales,
    offs, hz, n1, n2, n3, n4, out_0, out_1, out_2,
):
    nc = tc.nc
    with ExitStack() as ctx:
        lists = ctx.enter_context(tc.tile_pool(name="lists", bufs=1))
        sb = ctx.enter_context(tc.tile_pool(name="sb", bufs=1))
        ps = ctx.enter_context(tc.psum_pool(name="ps", bufs=1))

        def load_list(name, src):
            tile = lists.tile([P, src.shape[1]], U16, name=name)
            nc.sync.dma_start(tile[:], src)
            return tile

        x_scale_rows = sb.tile([P, T], U8, name="x_scale_rows", tag="early", align_bytes=64)
        nc.gpsimd.memset(x_scale_rows[:].bitcast(I32), 0)
        nc.sync.dma_start(x_scale_rows[0:P:8, :].bitcast(I32), x_scales[0].bitcast(I32))
        hz_t = load_list("hz_t", hz)
        offs_t = load_list("offs_t", offs)
        w_raw = [sb.tile([P, 2 * H], U8, name="w_raw%d" % i, align_bytes=64) for i in range(2)]
        w_scale_in = sb.tile([16, 2 * H], U8, name="w_scale_in", tag="staged", align_bytes=64)
        nc.scalar.dma_start(w_scale_in[:, :H].bitcast(I32), w1_scales[0].bitcast(I32))
        nc.scalar.dma_start(w_scale_in[:, H:].bitcast(I32), w2_scales[0].bitcast(I32))
        nc.sync.dma_start(w_raw[0][:].bitcast(I32), w1_words[0].bitcast(I32))
        x_table = sb.tile([P, T], I32, name="x_table", align_bytes=64)
        x_columns = x_words[0].rearrange("p n t -> p (n t)").bitcast(I32)
        nc.sync.dma_start(x_table[:, :X_FIRST], x_columns[:, :X_FIRST])
        nc.sync.dma_start(x_table[:, X_FIRST:], x_columns[:, X_FIRST:])
        nc.sync.dma_start(w_raw[1][:].bitcast(I32), w2_words[0].bitcast(I32))
        w_scale_rows = sb.tile([P, 2 * H], U8, name="w_scale_rows", align_bytes=64)
        nc.vector.memset(w_scale_rows[:].bitcast(I32), 0)
        for q in range(4):
            nc.sync.dma_start(w_scale_rows[32 * q : 32 * q + 4, :].bitcast(I32), w_scale_in[4 * q : 4 * q + 4, :].bitcast(I32))

        picked_plane = sb.tile([P, 2 * S], U8, name="picked_plane", align_bytes=64)
        picked_bytes = sb.tile([P, 2 * S], U8, name="picked_bytes", align_bytes=64)
        nc.vector.tensor_copy(picked_bytes[:, S:], x_scale_rows[:].indirect(hz_t[:]))
        nc.vector.tensor_copy(picked_bytes[:, :S], x_scale_rows[:].indirect(offs_t[:]))
        for b in range(4):
            nc.sync.dma_start(picked_plane[b:P:32, :].bitcast(I32), picked_bytes[8 * b : P : 32, :].bitcast(I32))
        n1_t = load_list("n1_t", n1)
        n2_t = load_list("n2_t", n2)
        gain_in = sb.tile([P, PACK], F32, name="gain_in")
        nc.gpsimd.dma_start(gain_in[:], gn.rearrange("(p t) o -> p (t o)", t=PACK))
        n3_t = load_list("n3_t", n3)
        n4_t = load_list("n4_t", n4)
        gain = sb.tile([P, PACK], F32, name="gain")
        nc.scalar.activation(gain[:], gain_in[:], COPY, scale=0.75)

        w_codes = [sb.tile([P, 2 * H], U8, name="w_codes%d" % i, align_bytes=64) for i in range(3)]

        def deal_words(i):
            nc.scalar.copy(
                w_codes[i][:].bitcast(U16).rearrange("p (t m) -> p t m", t=PACK),
                w_raw[i][:].bitcast(U16).rearrange("p (m t) -> p t m", t=PACK),
            )

        def deal_scales(plane, rows):
            nc.vector.tensor_copy(
                plane[:].rearrange("p (i t m) -> p i t m", m=P, t=PACK),
                rows.rearrange("p (i m t) -> p i t m", m=P, t=PACK),
            )

        for i in range(2):
            deal_words(i)
        w12_plane = sb.tile([P, 2 * H], U8, name="w12_plane", align_bytes=64)
        w3_plane = sb.tile([P, N], U8, name="w3_plane", align_bytes=64)
        w_planes = (w12_plane[:, :H], w12_plane[:, H:], w3_plane[:])
        deal_scales(w12_plane, w_scale_rows[:])

        words_by_offs = sb.tile([P, S], U32, name="words_by_offs", align_bytes=64)
        words_by_hz = sb.tile([P, S], U32, name="words_by_hz", tag="staged", align_bytes=64)
        nc.vector.tensor_copy(words_by_offs[:], x_table[:].bitcast(U32).indirect(offs_t[:]))
        nc.vector.tensor_copy(words_by_hz[:], x_table[:].bitcast(U32).indirect(hz_t[:]))
        w3_raw = sb.tile([P, 2 * N], U8, name="w3_raw", tag="early", align_bytes=64)
        w_raw.append(w3_raw)
        nc.sync.dma_start(w3_raw[:].bitcast(I32), w3_words[0].bitcast(I32))
        for q in range(4):
            nc.sync.dma_start(w_scale_rows[32 * q : 32 * q + 4, :N].bitcast(I32), w3_scales[0, 4 * q : 4 * q + 4, :].bitcast(I32))

        def product(out, i, t, codes, plane):
            nc.tensor.matmul_mx(
                out=out,
                lhsT=w_codes[i][:, 2 * P * t : 2 * P * (t + 1)].bitcast(FP4X4),
                lhsT_scale=w_planes[i][:, P * t : P * (t + 1)],
                rhs=codes.bitcast(FP8X4),
                rhs_scale=plane,
                start=True,
                stop=True,
            )

        y_d_n2 = sb.tile([P, PACK, S], F32, name="y_d_n2")
        y_n1_d = sb.tile([P, PACK, S], F32, name="y_n1_d")
        y_sb = [sb.tile([P, 2 * S], F32, name="y_sb%d" % t) for t in range(PACK)]
        d_sb = [sb.tile([P, 2 * S], F32, name="d_sb%d" % t) for t in range(PACK)]
        for t in range(PACK):
            y_ps = ps.tile([P, S], F32, name="y_ps", tag="y%d" % t)
            d_ps = ps.tile([P, S], F32, name="d_ps", tag="d%d" % t)
            product(y_ps[:], 0, t, words_by_offs[:], picked_plane[:, :S])
            product(d_ps[:], 1, t, words_by_hz[:], picked_plane[:, S:])
            y_n1 = sb.tile([P, S], F32, name="y_n1%d" % t)
            nc.scalar.activation(y_sb[t][:, :S], y_ps[:], COPY, scale=gain[:, t : t + 1])
            if t == 0:
                nc.vector.tensor_copy(d_sb[t][:, :S], d_ps[:])
            else:
                nc.scalar.copy(d_sb[t][:, :S], d_ps[:])
            nc.scalar.activation(y_n1[:], y_sb[t][:].indirect(n1_t[:]), COPY)
            nc.vector.tensor_tensor(y_d_n2[:, t, :], d_sb[t][:].indirect(n2_t[:]), y_sb[t][:, :S], MULT)
            nc.vector.tensor_tensor(y_n1_d[:, t, :], y_n1[:], d_sb[t][:, :S], MULT)
        deal_words(2)
        deal_scales(w3_plane, w_scale_rows[:, :N])

        h_sb = [sb.tile([P, S], F32, name="h_sb%d" % t) for t in range(PACK)]
        z16 = [sb.tile([P, HALF, PACK], BF16, name="z16_%d" % c, align_bytes=64) for c in range(2)]
        for c in range(2):
            cols = slice(c * HALF, (c + 1) * HALF)
            nc.vector.tensor_tensor(
                z16[c][:].rearrange("p (c i) t -> p c t i", i=4),
                y_d_n2[:, :, cols].rearrange("p t (c i) -> p c t i", i=4),
                y_n1_d[:, :, cols].rearrange("p t (c i) -> p c t i", i=4),
                SUB,
            )
        z_codes = [sb.tile([P, HALF], U32, name="z_codes%d" % c, align_bytes=64) for c in range(2)]
        z_plane = [sb.tile([P, HALF], U8, name="z_plane%d" % c, align_bytes=64) for c in range(2)]
        for c in range(2):
            nc.vector.quantize_mx(z_codes[c][:].bitcast(FP8X4), z_plane[c][:], z16[c][:].rearrange("p c t -> p (c t)"))

        out_rows = out_0.rearrange("(p t) j -> p t j", t=PACK)
        res = [sb.tile([P, S], F32, name="res%d" % t) for t in range(PACK)]
        for pair in ((0, 1), (2, 3)):
            pa, minus_pb = {}, {}
            for t in pair:
                pa[t] = sb.tile([P, W], F32, name="pa%d" % t)
                minus_pb[t] = sb.tile([P, W], F32, name="minus_pb%d" % t)
                for c in range(2):
                    h_ps = ps.tile([P, HALF], F32, name="h_ps", tag=H_BANKS[t][c])
                    product(h_ps[:], 2, t, z_codes[c][:], z_plane[c][:])
                    if (t, c) == (0, 1):
                        nc.vector.tensor_copy(h_sb[t][:, HALF:], h_ps[:])
                    else:
                        nc.scalar.copy(h_sb[t][:, c * HALF : (c + 1) * HALF], h_ps[:])
                nc.scalar.activation(pa[t][:], h_sb[t][:].indirect(n3_t[:]), COPY)
                if t == 0:
                    nc.vector.tensor_scalar(minus_pb[t][:], h_sb[t][:].indirect(n4_t[:]), -1.0, 0.0, MULT, ADD)
                else:
                    nc.scalar.activation(minus_pb[t][:], h_sb[t][:].indirect(n4_t[:]), COPY, scale=-1.0)
                nc.vector.tensor_tensor(res[t][:].indirect(n4_t[:]), pa[t][:], minus_pb[t][:], ADD)
            for t in pair:
                pa34 = sb.tile([P, W], F32, name="pa34_%d" % t)
                pb34 = sb.tile([P, W], F32, name="pb34_%d" % t)
                nc.scalar.activation(pa34[:], pa[t][:], COPY, scale=0.75)
                nc.scalar.activation(pb34[:], minus_pb[t][:], COPY, scale=-0.75)
                nc.vector.tensor_tensor(res[t][:].indirect(n3_t[:]), pa34[:], pb34[:], ADD)
                nc.sync.dma_start(out_rows[:, t, :], res[t][:])

        out16 = sb.tile([P, PACK, S], BF16, name="out16", align_bytes=64)
        for t in range(PACK - 1):
            nc.scalar.copy(out16[:, t, :], res[t][:])
        shares = ((nc.vector.tensor_copy, slice(0, OUT_VECTOR)), (nc.scalar.copy, slice(OUT_VECTOR, S)))
        woven = []
        for c, (copy, cols) in enumerate(shares):
            share = sb.tile([P, cols.stop - cols.start, PACK], BF16, name="woven%d" % c, align_bytes=64)
            woven.append(share)
            copy(out16[:, PACK - 1, cols], res[PACK - 1][:, cols])
            copy(
                share[:].rearrange("p (c i) t -> p c t i", i=4),
                out16[:, :, cols].rearrange("p t (c i) -> p c t i", i=4),
            )
        out_plane = sb.tile([P, S], U8, name="out_plane", align_bytes=64)
        out_words = out_1[0].rearrange("p n t -> p (n t)").bitcast(I32)
        for c, (copy, cols) in enumerate(shares):
            out_codes = sb.tile([P, cols.stop - cols.start], I32, name="out_codes%d" % c, align_bytes=64)
            nc.vector.quantize_mx(out_codes[:].bitcast(FP8X4), out_plane[:, cols], woven[c][:].rearrange("p c t -> p (c t)"))
            nc.sync.dma_start(out_words[:, cols], out_codes[:])
        for q in range(4):
            queue = (nc.scalar, nc.sync)[q % 2]
            queue.dma_start(out_2[0, 4 * q : 4 * q + 4, :].bitcast(I32), out_plane[32 * q : 32 * q + 4, :].bitcast(I32))
